import numpy as np
import ml_dtypes


def mxq(x, axis, fmt="e4m3"):
    dtype, down = {"e4m3": (ml_dtypes.float8_e4m3fn, 7), "e5m2": (ml_dtypes.float8_e5m2, 14)}[fmt]
    v = np.moveaxis(np.asarray(x, np.float32).astype(ml_dtypes.bfloat16).astype(np.float64), axis, -1)
    blocks = v.reshape(v.shape[:-1] + (-1, 32))
    amax = np.abs(blocks).max(-1, keepdims=True)
    byte = np.maximum(np.where(amax > 0, np.frexp(amax)[1] - 1 + 127, 0) - down, 1)
    scale = np.exp2(byte - 127.0)
    codes = (blocks / scale).astype(np.float32).astype(dtype).astype(np.float64)
    return np.moveaxis((codes * scale).reshape(v.shape), -1, axis)


WIDE = False


def mx_kscale(k):
    if not WIDE:
        return np.ones(k)
    levels = np.array([10, -10, 5, -5, 0])
    if k % 512:
        return np.exp2(np.random.permutation(np.resize(levels, k // 32))).repeat(32)
    a = np.empty((k // 512, 16))
    for p in range(k // 512):
        a[p, :8] = np.random.permutation(np.resize(levels, 8))
        for g in range(8):
            far = levels[np.abs(levels - a[p, g]) >= 10]
            a[p, g + 8] = far[np.random.randint(len(far))]
    return np.exp2(a.ravel()).repeat(32)


def f64(x):
    return np.asarray(x).astype(np.float64)


def striped(idx):
    return np.tile(idx.reshape(-1, 16).T, (8, 1)).astype(np.uint16)


def unstriped(offs):
    return offs[:16].T.reshape(-1).astype(np.int64)


def striped8(idx):
    return np.concatenate([v.reshape(-1, 16).T for v in idx]).astype(np.uint16)


def unstriped8(offs):
    return np.stack([offs[16 * g:16 * g + 16].T.reshape(-1) for g in range(8)]).astype(np.int64)


E2M1 = np.array([0.0, 0.5, 1.0, 1.5, 2.0, 3.0, 4.0, 6.0, -0.0, -0.5, -1.0, -1.5, -2.0, -3.0, -4.0, -6.0])


def pack_weight(w, fmt):
    k, n = w.shape
    w = f64(np.asarray(w, np.float32).astype(ml_dtypes.bfloat16)).reshape(k // 32, 32, n)
    amax = np.abs(w).max(1)
    if fmt == "e4m3":
        byte = np.frexp(amax)[1] - 1 + 127 - 7
    else:
        mant, ex = np.frexp(amax / 6.0)
        byte = np.where(mant > 0.5, ex, ex - 1) + 127
    byte = np.clip(np.where(amax > 0, byte, 1), 1, 254)
    scaled = (w * np.exp2(127.0 - byte)[:, None, :]).reshape(k, n).astype(np.float32)
    by_word = np.ascontiguousarray(scaled.reshape(k // 512, 128, 4, n).transpose(0, 1, 3, 2))
    if fmt == "e4m3":
        words = by_word.astype(ml_dtypes.float8_e4m3fn).view(np.uint8)
    else:
        c = by_word.astype(ml_dtypes.float4_e2m1fn).view(np.uint8) & 0xF
        words = (c[..., 0::2] | (c[..., 1::2] << 4)).reshape(k // 512, 128, 2 * n)
    return np.ascontiguousarray(words), np.ascontiguousarray(byte.astype(np.uint8).reshape(k // 512, 16, n))


def unpack_weight(words, scales, fmt):
    g, _, n = scales.shape
    words = np.ascontiguousarray(words).reshape(g, 128, n, -1)
    if fmt == "e4m3":
        vals = words.view(ml_dtypes.float8_e4m3fn).astype(np.float64)
    else:
        nib = np.empty((g, 128, n, 4), np.uint8)
        nib[..., 0::2] = words & 0xF
        nib[..., 1::2] = words >> 4
        vals = E2M1[nib]
    vals = vals * np.repeat(np.exp2(scales.astype(np.float64) - 127.0), 8, axis=1)[..., None]
    return vals.transpose(0, 1, 3, 2).reshape(g * 512, n)


def pack_table(v):
    words, scales = pack_weight(v, "e4m3")
    return np.concatenate([words.reshape(words.shape[0], -1), scales.reshape(scales.shape[0], -1)], axis=1)


def unpack_table(tab):
    g, t = tab.shape[0], tab.shape[1] // 528
    return unpack_weight(tab[:, :512 * t].reshape(g, 128, t, 4), tab[:, 512 * t:].reshape(g, 16, t), "e4m3")


def gelu(v):
    return 0.5 * v * (1.0 + np.tanh(np.sqrt(2.0 / np.pi) * (v + 0.044715 * v**3)))


K, M, T, S = 1024, 1024, 4096, 2048


def setup_inputs():
    n = np.random.standard_normal
    s = mx_kscale(K)[:, None]
    u = mx_kscale(512)[:, None]
    p_w4 = pack_weight(n((K, M)) / np.sqrt(K) / s, "e2m1")
    return {
        "tab": pack_table(n((K, T)) * s),
        "w4_words": p_w4[0],
        "w4_scales": p_w4[1],
        "down": (n((K, 512)) / np.sqrt(K) / s * u.T).astype(np.float32),
        "up": (0.5 * n((512, M)) / np.sqrt(512) / u).astype(np.float32),
        "b": (0.3 * n(1024)).astype(np.float32),
        "wgo": np.repeat(np.random.uniform(0.5, 2.0, (8, S)), 16, axis=0).astype(np.float32),
        "offs": striped(np.random.permutation(T)[:S]),
        "offs2": striped8(np.stack([np.random.permutation(T)[:S] for _ in range(8)])),
    }


def reference(tab, w4_words, w4_scales, down, up, b, wgo, offs, offs2):
    tab_ = unpack_table(tab)[:, unstriped(offs)]
    w4_ = unpack_weight(w4_words, w4_scales, "e2m1")
    down_ = mxq(f64(down), 0, "e4m3")
    up_ = mxq(f64(up), 0, "e4m3")
    h_ = mxq(down_.T @ tab_, 0, "e4m3")
    y = w4_.T @ tab_ + up_.T @ h_
    place = unstriped8(offs2)[np.arange(M) % 128 // 16]
    out = np.zeros((M, T))
    out[np.arange(M)[:, None], place] = f64(wgo)[np.arange(M) % 128] * (gelu(y + f64(b)[:, None]))
    return out

@@ -1,0 +1,228 @@
+from contextlib import ExitStack
+
+import concourse.mybir as mybir
+
+K, M, T, S, R = 1024, 1024, 4096, 2048, 512
+FLOPS = 2 * S * (K * M + K * R + R * M)
+
+F32 = mybir.dt.float32
+BF16 = mybir.dt.bfloat16
+I32 = mybir.dt.int32
+U32 = mybir.dt.uint32
+U16 = mybir.dt.uint16
+U8 = mybir.dt.uint8
+FP8X4 = mybir.dt.float8_e4m3fn_x4
+FP4X4 = mybir.dt.float4_e2m1fn_x4
+GELU = mybir.ActivationFunctionType.Gelu_apprx_tanh
+MULT = mybir.AluOpType.mult
+
+P = 128
+PACK = 4
+K_PASS = P * PACK
+PASSES = K // K_PASS
+CHUNK = 512
+CHUNKS = S // CHUNK
+ROW_TILES = M // P
+UP_HEAD = 256
+
+
+def tile_list_tabhs_l_gelu_kernel(
+    tc, tab, w4_words, w4_scales, down, up, b, wgo, offs, offs2, out
+):
+    nc = tc.nc
+    with ExitStack() as ctx:
+        keep = ctx.enter_context(tc.tile_pool(name="keep", bufs=1))
+        ring = ctx.enter_context(tc.tile_pool(name="ring", bufs=2))
+        psum = ctx.enter_context(tc.psum_pool(name="psum", bufs=4))
+
+        def held(name, cols, dtype):
+            return keep.tile([P, cols], dtype, name=name, align_bytes=64)
+
+        pick = keep.tile([P, S // 16], U16, name="pick")
+        place = keep.tile([P, S // 16], U16, name="place")
+        tab_scales = held("tab_scales", T, U8)
+        tab_words = [held("tab_words%d" % a, T, U32) for a in range(PASSES)]
+        down_raw = [held("down_raw%d" % a, PACK * R, F32) for a in range(PASSES)]
+        w4_sc = held("w4_sc", PASSES * M, U8)
+        w4_w = held("w4_w", PASSES * 2 * M, U8)
+        up_cols = [(0, UP_HEAD), (UP_HEAD, 512), (512, M)]
+        up_raw = [held("up_raw%d" % i, PACK * (c1 - c0), F32) for i, (c0, c1) in enumerate(up_cols)]
+        wgo_sb = held("wgo_sb", S, F32)
+        bias = held("bias", ROW_TILES, F32)
+        v_scales = held("v_scales", S, U8)
+        v_scales1 = held("v_scales1", S, U8)
+        pages = [held("page%d" % i, T, F32) for i in range(2)]
+        warm = held("warm", 16, F32)
+
+        nc.vector.memset(tab_scales[:].bitcast(I32), 0)
+        nc.vector.memset(warm[:, 0:8], 0.0)
+        nc.vector.memset(w4_sc[:].bitcast(I32), 0)
+        nc.vector.memset(v_scales1[:].bitcast(I32), 0)
+        nc.scalar.activation(warm[:, 8:16], warm[:, 0:8], GELU)
+
+        def load_words(a):
+            src = tab[a, 0 : K_PASS * T].rearrange("(p x) -> p x", p=P).bitcast(I32)
+            nc.sync.dma_start(tab_words[a][:].bitcast(I32), src)
+
+        def load_down(a):
+            src = down[a * K_PASS : (a + 1) * K_PASS, :].rearrange("(p j) r -> p (j r)", j=PACK)
+            nc.sync.dma_start(down_raw[a][:], src)
+
+        def load_up(i):
+            c0, c1 = up_cols[i]
+            src = up[:, c0:c1].rearrange("(p j) n -> p j n", j=PACK)
+            nc.sync.dma_start(up_raw[i][:].rearrange("p (j n) -> p j n", j=PACK), src)
+
+        nc.sync.dma_start(pick[:], offs)
+        for q in range(4):
+            rows = tab[:, K_PASS * T + 4 * q * T : K_PASS * T + 4 * (q + 1) * T]
+            nc.sync.dma_start(
+                tab_scales[32 * q : 32 * q + 8, :].bitcast(I32),
+                rows.rearrange("a (r t) -> a r t", r=4).bitcast(I32),
+            )
+        load_down(0)
+        load_words(0)
+        load_down(1)
+        load_words(1)
+        for q in range(4):
+            nc.sync.dma_start(
+                w4_sc[32 * q : 32 * q + 4, :].bitcast(I32).rearrange("r (a n) -> r a n", a=PASSES),
+                w4_scales[:, 4 * q : 4 * q + 4, :].bitcast(I32).rearrange("a r n -> r a n"),
+            )
+        load_up(0)
+        nc.sync.dma_start(
+            w4_w[:].bitcast(I32).rearrange("p (a n) -> p a n", a=PASSES),
+            w4_words.bitcast(I32).rearrange("a p n -> p a n"),
+        )
+        nc.sync.dma_start(place[:], offs2)
+        nc.sync.dma_start(wgo_sb[:, 0:CHUNK], wgo[:, 0:CHUNK])
+        with nc.allow_non_contiguous_dma(reason="one bias value a partition"):
+            nc.sync.dma_start(bias[:], b.rearrange("(c p) -> p c", p=P))
+        nc.sync.dma_start(wgo_sb[:, CHUNK:S], wgo[:, CHUNK:S])
+        load_up(1)
+        load_up(2)
+
+        for page in pages:
+            nc.vector.memset(page[:], 0.0)
+
+        nc.vector.tensor_copy(v_scales[:], tab_scales[:].indirect(pick[:]))
+        nc.sync.dma_start(v_scales1[0 : P - 4, :].bitcast(I32), v_scales[4:P, :].bitcast(I32))
+
+        down_q = [held("down_q%d" % a, R, U32) for a in range(PASSES)]
+        down_s = [held("down_s%d" % a, R, U8) for a in range(PASSES)]
+
+        def quantise_down(a):
+            grouped = held("down_bf%d" % a, PACK * R, BF16)
+            nc.scalar.copy(
+                grouped[:].rearrange("p (t m j) -> p m t j", t=PACK, j=PACK),
+                down_raw[a][:].rearrange("p (j m t) -> p m t j", j=PACK, t=PACK),
+            )
+            nc.vector.quantize_mx(down_q[a][:].bitcast(FP8X4), down_s[a][:], grouped[:])
+
+        up_q = held("up_q", M, U32)
+        up_s = held("up_s", M, U8)
+
+        def quantise_up(i):
+            c0, c1 = up_cols[i]
+            grouped = held("up_bf%d" % i, PACK * (c1 - c0), BF16)
+            nc.scalar.copy(
+                grouped[:].rearrange("p (c i j) -> p c j i", i=4, j=PACK),
+                up_raw[i][:].rearrange("p (j c i) -> p c j i", i=4, j=PACK),
+            )
+            nc.vector.quantize_mx(up_q[:, c0:c1].bitcast(FP8X4), up_s[:, c0:c1], grouped[:])
+
+        v_words0 = held("v_words0", S, U32)
+        v_words1 = [held("v_words1_%d" % c, CHUNK, U32) for c in range(CHUNKS)]
+
+        def list_cols(c):
+            return slice(c * CHUNK // 16, (c + 1) * CHUNK // 16)
+
+        def v_words(a, j0, j1):
+            if a == 0:
+                return v_words0[:, j0:j1].bitcast(FP8X4)
+            c = j0 // CHUNK
+            return v_words1[c][:, j0 - c * CHUNK : j1 - c * CHUNK].bitcast(FP8X4)
+
+        quantise_down(0)
+        nc.vector.tensor_copy(v_words0[:], tab_words[0][:].indirect(pick[:]))
+        quantise_down(1)
+        for c in range(CHUNKS):
+            nc.vector.tensor_copy(v_words1[c][:], tab_words[1][:].indirect(pick[:, list_cols(c)]))
+        quantise_up(0)
+
+        h_q = [held("h_q%d" % c, CHUNK, U32) for c in range(CHUNKS)]
+        h_s = [held("h_s%d" % c, CHUNK, U8) for c in range(CHUNKS)]
+
+        def make_h(c):
+            grouped = ring.tile([P, PACK * CHUNK], BF16, name="h_bf", align_bytes=64)
+            for u in range(CHUNK // P):
+                j0 = c * CHUNK + u * P
+                bank = psum.tile([P, PACK, P], F32, name="h_bank")
+                for t in range(PACK):
+                    for a in range(PASSES):
+                        nc.tensor.matmul_mx(
+                            out=bank[:, t, :],
+                            lhsT=down_q[a][:, t * P : (t + 1) * P].bitcast(FP8X4),
+                            lhsT_scale=down_s[a][:, t * P : (t + 1) * P],
+                            rhs=v_words(a, j0, j0 + P),
+                            rhs_scale=v_scales[4 * a : P, j0 : j0 + P],
+                            start=(a == 0),
+                            stop=(a == PASSES - 1),
+                        )
+                nc.scalar.copy(
+                    grouped[:, u * PACK * P : (u + 1) * PACK * P].rearrange("p (n t) -> p n t", t=PACK),
+                    bank[:].rearrange("p t n -> p n t"),
+                )
+            nc.vector.quantize_mx(h_q[c][:].bitcast(FP8X4), h_s[c][:], grouped[:])
+
+        def make_y(i, c, act):
+            j0, j1 = c * CHUNK, (c + 1) * CHUNK
+            n0, n1 = i * P, (i + 1) * P
+            bank = psum.tile([P, CHUNK], F32, name="y_bank")
+            for a in range(PASSES):
+                plane = v_scales if a == 0 else v_scales1
+                nc.tensor.matmul_mx(
+                    out=bank[:],
+                    lhsT=w4_w[:, 2 * (a * M + n0) : 2 * (a * M + n1)].bitcast(FP4X4),
+                    lhsT_scale=w4_sc[:, a * M + n0 : a * M + n1],
+                    rhs=v_words(a, j0, j1),
+                    rhs_scale=plane[:, j0:j1],
+                    start=(a == 0),
+                    stop=False,
+                )
+            nc.tensor.matmul_mx(
+                out=bank[:],
+                lhsT=up_q[:, n0:n1].bitcast(FP8X4),
+                lhsT_scale=up_s[:, n0:n1],
+                rhs=h_q[c][:].bitcast(FP8X4),
+                rhs_scale=h_s[c][:],
+                start=False,
+                stop=True,
+            )
+            nc.scalar.activation(act[:, j0:j1], bank[:], GELU, bias=bias[:, i : i + 1])
+
+        def store(i, pieces):
+            width = T // pieces
+            for s in range(pieces):
+                cols = slice(s * width, (s + 1) * width)
+                nc.sync.dma_start(out[i * P : (i + 1) * P, cols], pages[i % 2][:, cols])
+
+        act = ring.tile([P, S], F32, name="act")
+        make_h(0)
+        for c in range(CHUNKS):
+            if c + 1 < CHUNKS:
+                make_h(c + 1)
+            make_y(0, c, act)
+            cols = slice(c * CHUNK, (c + 1) * CHUNK)
+            nc.vector.tensor_tensor(
+                pages[0][:].indirect(place[:, list_cols(c)]), act[:, cols], wgo_sb[:, cols], MULT
+            )
+        store(0, 1)
+        quantise_up(1)
+        quantise_up(2)
+        for i in range(1, ROW_TILES):
+            act = ring.tile([P, S], F32, name="act")
+            for c in range(CHUNKS):
+                make_y(i, c, act)
+            nc.vector.tensor_tensor(pages[i % 2][:].indirect(place[:]), act[:], wgo_sb[:], MULT)
+            store(i, 2 if i == ROW_TILES - 1 else 1)

@@ -54,10 +54,10 @@ def tile_list_tabhs_l_gelu_kernel(
         pages = [held("page%d" % i, T, F32) for i in range(2)]
         warm = held("warm", 16, F32)
 
-        nc.vector.memset(tab_scales[:].bitcast(I32), 0)
-        nc.vector.memset(warm[:, 0:8], 0.0)
-        nc.vector.memset(w4_sc[:].bitcast(I32), 0)
-        nc.vector.memset(v_scales1[:].bitcast(I32), 0)
+        nc.gpsimd.memset(tab_scales[:].bitcast(I32), 0)
+        nc.gpsimd.memset(warm[:, 0:8], 0.0)
+        nc.gpsimd.memset(w4_sc[:].bitcast(I32), 0)
+        nc.gpsimd.memset(v_scales1[:].bitcast(I32), 0)
         nc.scalar.activation(warm[:, 8:16], warm[:, 0:8], GELU)
 
         def load_words(a):
@@ -74,14 +74,17 @@ def tile_list_tabhs_l_gelu_kernel(
             nc.sync.dma_start(up_raw[i][:].rearrange("p (j n) -> p j n", j=PACK), src)
 
         nc.sync.dma_start(pick[:], offs)
+        nc.sync.dma_start(place[:], offs2)
+        with nc.allow_non_contiguous_dma(reason="one bias value a partition"):
+            nc.sync.dma_start(bias[:], b.rearrange("(c p) -> p c", p=P))
         for q in range(4):
             rows = tab[:, K_PASS * T + 4 * q * T : K_PASS * T + 4 * (q + 1) * T]
             nc.sync.dma_start(
                 tab_scales[32 * q : 32 * q + 8, :].bitcast(I32),
                 rows.rearrange("a (r t) -> a r t", r=4).bitcast(I32),
             )
-        load_down(0)
         load_words(0)
+        load_down(0)
         load_down(1)
         load_words(1)
         for q in range(4):
@@ -94,19 +97,17 @@ def tile_list_tabhs_l_gelu_kernel(
             w4_w[:].bitcast(I32).rearrange("p (a n) -> p a n", a=PASSES),
             w4_words.bitcast(I32).rearrange("a p n -> p a n"),
         )
-        nc.sync.dma_start(place[:], offs2)
         nc.sync.dma_start(wgo_sb[:, 0:CHUNK], wgo[:, 0:CHUNK])
-        with nc.allow_non_contiguous_dma(reason="one bias value a partition"):
-            nc.sync.dma_start(bias[:], b.rearrange("(c p) -> p c", p=P))
         nc.sync.dma_start(wgo_sb[:, CHUNK:S], wgo[:, CHUNK:S])
         load_up(1)
         load_up(2)
 
         for page in pages:
-            nc.vector.memset(page[:], 0.0)
+            for x in range(0, T, 1024):
+                nc.gpsimd.memset(page[:, x : x + 1024], 0.0)
 
         nc.vector.tensor_copy(v_scales[:], tab_scales[:].indirect(pick[:]))
-        nc.sync.dma_start(v_scales1[0 : P - 4, :].bitcast(I32), v_scales[4:P, :].bitcast(I32))
+        nc.gpsimd.dma_start(v_scales1[0 : P - 4, :].bitcast(I32), v_scales[4:P, :].bitcast(I32))
 
         down_q = [held("down_q%d" % a, R, U32) for a in range(PASSES)]
         down_s = [held("down_s%d" % a, R, U8) for a in range(PASSES)]
@@ -143,8 +144,8 @@ def tile_list_tabhs_l_gelu_kernel(
             c = j0 // CHUNK
             return v_words1[c][:, j0 - c * CHUNK : j1 - c * CHUNK].bitcast(FP8X4)
 
-        quantise_down(0)
         nc.vector.tensor_copy(v_words0[:], tab_words[0][:].indirect(pick[:]))
+        quantise_down(0)
         quantise_down(1)
         for c in range(CHUNKS):
             nc.vector.tensor_copy(v_words1[c][:], tab_words[1][:].indirect(pick[:, list_cols(c)]))
@@ -155,24 +156,27 @@ def tile_list_tabhs_l_gelu_kernel(
 
         def make_h(c):
             grouped = ring.tile([P, PACK * CHUNK], BF16, name="h_bf", align_bytes=64)
-            for u in range(CHUNK // P):
+            banks = [psum.tile([P, PACK, P], F32, name="h_bank") for u in range(CHUNK // P)]
+            order = [(a, u) for a in range(PASSES) for u in range(CHUNK // P)]
+            if c > 0:
+                order = [(a, u) for u in range(CHUNK // P) for a in range(PASSES)]
+            for a, u in order:
                 j0 = c * CHUNK + u * P
-                bank = psum.tile([P, PACK, P], F32, name="h_bank")
                 for t in range(PACK):
-                    for a in range(PASSES):
-                        nc.tensor.matmul_mx(
-                            out=bank[:, t, :],
-                            lhsT=down_q[a][:, t * P : (t + 1) * P].bitcast(FP8X4),
-                            lhsT_scale=down_s[a][:, t * P : (t + 1) * P],
-                            rhs=v_words(a, j0, j0 + P),
-                            rhs_scale=v_scales[4 * a : P, j0 : j0 + P],
-                            start=(a == 0),
-                            stop=(a == PASSES - 1),
-                        )
-                nc.scalar.copy(
-                    grouped[:, u * PACK * P : (u + 1) * PACK * P].rearrange("p (n t) -> p n t", t=PACK),
-                    bank[:].rearrange("p t n -> p n t"),
-                )
+                    nc.tensor.matmul_mx(
+                        out=banks[u][:, t, :],
+                        lhsT=down_q[a][:, t * P : (t + 1) * P].bitcast(FP8X4),
+                        lhsT_scale=down_s[a][:, t * P : (t + 1) * P],
+                        rhs=v_words(a, j0, j0 + P),
+                        rhs_scale=v_scales[4 * a : P, j0 : j0 + P],
+                        start=(a == 0 and t == 0),
+                        stop=(a == PASSES - 1 and t == PACK - 1),
+                    )
+                if a == PASSES - 1:
+                    nc.scalar.copy(
+                        grouped[:, u * PACK * P : (u + 1) * PACK * P].rearrange("p (n t) -> p n t", t=PACK),
+                        banks[u][:].rearrange("p t n -> p n t"),
+                    )
             nc.vector.quantize_mx(h_q[c][:].bitcast(FP8X4), h_s[c][:], grouped[:])
 
         def make_y(i, c, act):
@@ -207,22 +211,34 @@ def tile_list_tabhs_l_gelu_kernel(
                 cols = slice(s * width, (s + 1) * width)
                 nc.sync.dma_start(out[i * P : (i + 1) * P, cols], pages[i % 2][:, cols])
 
-        act = ring.tile([P, S], F32, name="act")
+        def scatter(i, act, c0, c1):
+            cols = slice(c0 * CHUNK, c1 * CHUNK)
+            lists = place[:, c0 * CHUNK // 16 : c1 * CHUNK // 16]
+            nc.vector.tensor_tensor(pages[i % 2][:].indirect(lists), act[:, cols], wgo_sb[:, cols], MULT)
+
+        act0 = ring.tile([P, S], F32, name="act")
+        act1 = ring.tile([P, S], F32, name="act")
         make_h(0)
-        for c in range(CHUNKS):
+        make_y(0, 0, act0)
+        scatter(0, act0, 0, 1)
+        make_h(1)
+        make_y(1, 0, act1)
+        scatter(1, act1, 0, 1)
+        for c in range(1, CHUNKS):
             if c + 1 < CHUNKS:
                 make_h(c + 1)
-            make_y(0, c, act)
-            cols = slice(c * CHUNK, (c + 1) * CHUNK)
-            nc.vector.tensor_tensor(
-                pages[0][:].indirect(place[:, list_cols(c)]), act[:, cols], wgo_sb[:, cols], MULT
-            )
+            make_y(0, c, act0)
+            scatter(0, act0, c, c + 1)
         store(0, 1)
         quantise_up(1)
         quantise_up(2)
-        for i in range(1, ROW_TILES):
+        for c in range(1, CHUNKS):
+            make_y(1, c, act1)
+        scatter(1, act1, 1, CHUNKS)
+        store(1, 1)
+        for i in range(2, ROW_TILES):
             act = ring.tile([P, S], F32, name="act")
             for c in range(CHUNKS):
                 make_y(i, c, act)
-            nc.vector.tensor_tensor(pages[i % 2][:].indirect(place[:]), act[:], wgo_sb[:], MULT)
+            scatter(i, act, 0, CHUNKS)
             store(i, 2 if i == ROW_TILES - 1 else 1)

from contextlib import ExitStack

import concourse.mybir as mybir

K, M, T, S, R = 1024, 1024, 4096, 2048, 512
FLOPS = 2 * S * (K * M + K * R + R * M)

F32 = mybir.dt.float32
BF16 = mybir.dt.bfloat16
I32 = mybir.dt.int32
U32 = mybir.dt.uint32
U16 = mybir.dt.uint16
U8 = mybir.dt.uint8
FP8X4 = mybir.dt.float8_e4m3fn_x4
FP4X4 = mybir.dt.float4_e2m1fn_x4
GELU = mybir.ActivationFunctionType.Gelu_apprx_tanh
MULT = mybir.AluOpType.mult

P = 128
PACK = 4
K_PASS = P * PACK
PASSES = K // K_PASS
CHUNK = 512
CHUNKS = S // CHUNK
ROW_TILES = M // P
UP_HEAD = 256


def tile_list_tabhs_l_gelu_kernel(
    tc, tab, w4_words, w4_scales, down, up, b, wgo, offs, offs2, out
):
    nc = tc.nc
    with ExitStack() as ctx:
        keep = ctx.enter_context(tc.tile_pool(name="keep", bufs=1))
        ring = ctx.enter_context(tc.tile_pool(name="ring", bufs=2))
        psum = ctx.enter_context(tc.psum_pool(name="psum", bufs=4))

        def held(name, cols, dtype):
            return keep.tile([P, cols], dtype, name=name, align_bytes=64)

        pick = keep.tile([P, S // 16], U16, name="pick")
        place = keep.tile([P, S // 16], U16, name="place")
        tab_scales = held("tab_scales", T, U8)
        tab_words = [held("tab_words%d" % a, T, U32) for a in range(PASSES)]
        down_raw = [held("down_raw%d" % a, PACK * R, F32) for a in range(PASSES)]
        w4_sc = held("w4_sc", PASSES * M, U8)
        w4_w = held("w4_w", PASSES * 2 * M, U8)
        up_cols = [(0, UP_HEAD), (UP_HEAD, 512), (512, M)]
        up_raw = [held("up_raw%d" % i, PACK * (c1 - c0), F32) for i, (c0, c1) in enumerate(up_cols)]
        wgo_sb = held("wgo_sb", S, F32)
        bias = held("bias", ROW_TILES, F32)
        v_scales = held("v_scales", S, U8)
        v_scales1 = held("v_scales1", S, U8)
        pages = [held("page%d" % i, T, F32) for i in range(2)]
        warm = held("warm", 16, F32)

        nc.gpsimd.memset(tab_scales[:].bitcast(I32), 0)
        nc.gpsimd.memset(warm[:, 0:8], 0.0)
        nc.gpsimd.memset(w4_sc[:].bitcast(I32), 0)
        nc.gpsimd.memset(v_scales1[:].bitcast(I32), 0)
        nc.scalar.activation(warm[:, 8:16], warm[:, 0:8], GELU)

        def load_words(a):
            src = tab[a, 0 : K_PASS * T].rearrange("(p x) -> p x", p=P).bitcast(I32)
            nc.sync.dma_start(tab_words[a][:].bitcast(I32), src)

        def load_down(a):
            src = down[a * K_PASS : (a + 1) * K_PASS, :].rearrange("(p j) r -> p (j r)", j=PACK)
            nc.sync.dma_start(down_raw[a][:], src)

        def load_up(i):
            c0, c1 = up_cols[i]
            src = up[:, c0:c1].rearrange("(p j) n -> p j n", j=PACK)
            nc.sync.dma_start(up_raw[i][:].rearrange("p (j n) -> p j n", j=PACK), src)

        nc.sync.dma_start(pick[:], offs)
        nc.sync.dma_start(place[:], offs2)
        with nc.allow_non_contiguous_dma(reason="one bias value a partition"):
            nc.sync.dma_start(bias[:], b.rearrange("(c p) -> p c", p=P))
        for q in range(4):
            rows = tab[:, K_PASS * T + 4 * q * T : K_PASS * T + 4 * (q + 1) * T]
            nc.sync.dma_start(
                tab_scales[32 * q : 32 * q + 8, :].bitcast(I32),
                rows.rearrange("a (r t) -> a r t", r=4).bitcast(I32),
            )
        load_words(0)
        load_down(0)
        load_down(1)
        load_words(1)
        for q in range(4):
            nc.sync.dma_start(
                w4_sc[32 * q : 32 * q + 4, :].bitcast(I32).rearrange("r (a n) -> r a n", a=PASSES),
                w4_scales[:, 4 * q : 4 * q + 4, :].bitcast(I32).rearrange("a r n -> r a n"),
            )
        load_up(0)
        nc.sync.dma_start(
            w4_w[:].bitcast(I32).rearrange("p (a n) -> p a n", a=PASSES),
            w4_words.bitcast(I32).rearrange("a p n -> p a n"),
        )
        nc.sync.dma_start(wgo_sb[:, 0:CHUNK], wgo[:, 0:CHUNK])
        nc.sync.dma_start(wgo_sb[:, CHUNK:S], wgo[:, CHUNK:S])
        load_up(1)
        load_up(2)

        for page in pages:
            for x in range(0, T, 1024):
                nc.gpsimd.memset(page[:, x : x + 1024], 0.0)

        nc.vector.tensor_copy(v_scales[:], tab_scales[:].indirect(pick[:]))
        nc.gpsimd.dma_start(v_scales1[0 : P - 4, :].bitcast(I32), v_scales[4:P, :].bitcast(I32))

        down_q = [held("down_q%d" % a, R, U32) for a in range(PASSES)]
        down_s = [held("down_s%d" % a, R, U8) for a in range(PASSES)]

        def quantise_down(a):
            grouped = held("down_bf%d" % a, PACK * R, BF16)
            nc.scalar.copy(
                grouped[:].rearrange("p (t m j) -> p m t j", t=PACK, j=PACK),
                down_raw[a][:].rearrange("p (j m t) -> p m t j", j=PACK, t=PACK),
            )
            nc.vector.quantize_mx(down_q[a][:].bitcast(FP8X4), down_s[a][:], grouped[:])

        up_q = held("up_q", M, U32)
        up_s = held("up_s", M, U8)

        def quantise_up(i):
            c0, c1 = up_cols[i]
            grouped = held("up_bf%d" % i, PACK * (c1 - c0), BF16)
            nc.scalar.copy(
                grouped[:].rearrange("p (c i j) -> p c j i", i=4, j=PACK),
                up_raw[i][:].rearrange("p (j c i) -> p c j i", i=4, j=PACK),
            )
            nc.vector.quantize_mx(up_q[:, c0:c1].bitcast(FP8X4), up_s[:, c0:c1], grouped[:])

        v_words0 = held("v_words0", S, U32)
        v_words1 = [held("v_words1_%d" % c, CHUNK, U32) for c in range(CHUNKS)]

        def list_cols(c):
            return slice(c * CHUNK // 16, (c + 1) * CHUNK // 16)

        def v_words(a, j0, j1):
            if a == 0:
                return v_words0[:, j0:j1].bitcast(FP8X4)
            c = j0 // CHUNK
            return v_words1[c][:, j0 - c * CHUNK : j1 - c * CHUNK].bitcast(FP8X4)

        nc.vector.tensor_copy(v_words0[:], tab_words[0][:].indirect(pick[:]))
        quantise_down(0)
        quantise_down(1)
        for c in range(CHUNKS):
            nc.vector.tensor_copy(v_words1[c][:], tab_words[1][:].indirect(pick[:, list_cols(c)]))
        quantise_up(0)

        h_q = [held("h_q%d" % c, CHUNK, U32) for c in range(CHUNKS)]
        h_s = [held("h_s%d" % c, CHUNK, U8) for c in range(CHUNKS)]

        def make_h(c):
            grouped = ring.tile([P, PACK * CHUNK], BF16, name="h_bf", align_bytes=64)
            banks = [psum.tile([P, PACK, P], F32, name="h_bank") for u in range(CHUNK // P)]
            order = [(a, u) for a in range(PASSES) for u in range(CHUNK // P)]
            if c > 0:
                order = [(a, u) for u in range(CHUNK // P) for a in range(PASSES)]
            for a, u in order:
                j0 = c * CHUNK + u * P
                for t in range(PACK):
                    nc.tensor.matmul_mx(
                        out=banks[u][:, t, :],
                        lhsT=down_q[a][:, t * P : (t + 1) * P].bitcast(FP8X4),
                        lhsT_scale=down_s[a][:, t * P : (t + 1) * P],
                        rhs=v_words(a, j0, j0 + P),
                        rhs_scale=v_scales[4 * a : P, j0 : j0 + P],
                        start=(a == 0 and t == 0),
                        stop=(a == PASSES - 1 and t == PACK - 1),
                    )
                if a == PASSES - 1:
                    nc.scalar.copy(
                        grouped[:, u * PACK * P : (u + 1) * PACK * P].rearrange("p (n t) -> p n t", t=PACK),
                        banks[u][:].rearrange("p t n -> p n t"),
                    )
            nc.vector.quantize_mx(h_q[c][:].bitcast(FP8X4), h_s[c][:], grouped[:])

        def make_y(i, c, act):
            j0, j1 = c * CHUNK, (c + 1) * CHUNK
            n0, n1 = i * P, (i + 1) * P
            bank = psum.tile([P, CHUNK], F32, name="y_bank")
            for a in range(PASSES):
                plane = v_scales if a == 0 else v_scales1
                nc.tensor.matmul_mx(
                    out=bank[:],
                    lhsT=w4_w[:, 2 * (a * M + n0) : 2 * (a * M + n1)].bitcast(FP4X4),
                    lhsT_scale=w4_sc[:, a * M + n0 : a * M + n1],
                    rhs=v_words(a, j0, j1),
                    rhs_scale=plane[:, j0:j1],
                    start=(a == 0),
                    stop=False,
                )
            nc.tensor.matmul_mx(
                out=bank[:],
                lhsT=up_q[:, n0:n1].bitcast(FP8X4),
                lhsT_scale=up_s[:, n0:n1],
                rhs=h_q[c][:].bitcast(FP8X4),
                rhs_scale=h_s[c][:],
                start=False,
                stop=True,
            )
            nc.scalar.activation(act[:, j0:j1], bank[:], GELU, bias=bias[:, i : i + 1])

        def store(i, pieces):
            width = T // pieces
            for s in range(pieces):
                cols = slice(s * width, (s + 1) * width)
                nc.sync.dma_start(out[i * P : (i + 1) * P, cols], pages[i % 2][:, cols])

        def scatter(i, act, c0, c1):
            cols = slice(c0 * CHUNK, c1 * CHUNK)
            lists = place[:, c0 * CHUNK // 16 : c1 * CHUNK // 16]
            nc.vector.tensor_tensor(pages[i % 2][:].indirect(lists), act[:, cols], wgo_sb[:, cols], MULT)

        act0 = ring.tile([P, S], F32, name="act")
        act1 = ring.tile([P, S], F32, name="act")
        make_h(0)
        make_y(0, 0, act0)
        scatter(0, act0, 0, 1)
        make_h(1)
        make_y(1, 0, act1)
        scatter(1, act1, 0, 1)
        for c in range(1, CHUNKS):
            if c + 1 < CHUNKS:
                make_h(c + 1)
            make_y(0, c, act0)
            scatter(0, act0, c, c + 1)
        store(0, 1)
        quantise_up(1)
        quantise_up(2)
        for c in range(1, CHUNKS):
            make_y(1, c, act1)
        scatter(1, act1, 1, CHUNKS)
        store(1, 1)
        for i in range(2, ROW_TILES):
            act = ring.tile([P, S], F32, name="act")
            for c in range(CHUNKS):
                make_y(i, c, act)
            scatter(i, act, 0, CHUNKS)
            store(i, 2 if i == ROW_TILES - 1 else 1)
